import numpy as np
import ml_dtypes


def mxq(x, axis, fmt="e4m3"):
    dtype, down = {"e4m3": (ml_dtypes.float8_e4m3fn, 7), "e5m2": (ml_dtypes.float8_e5m2, 14)}[fmt]
    v = np.moveaxis(np.asarray(x, np.float32).astype(ml_dtypes.bfloat16).astype(np.float64), axis, -1)
    blocks = v.reshape(v.shape[:-1] + (-1, 32))
    amax = np.abs(blocks).max(-1, keepdims=True)
    byte = np.maximum(np.where(amax > 0, np.frexp(amax)[1] - 1 + 127, 0) - down, 1)
    scale = np.exp2(byte - 127.0)
    codes = (blocks / scale).astype(np.float32).astype(dtype).astype(np.float64)
    return np.moveaxis((codes * scale).reshape(v.shape), -1, axis)


WIDE = False


def mx_kscale(k):
    if not WIDE:
        return np.ones(k)
    levels = np.array([30, -30])
    if k % 512:
        return np.exp2(np.random.permutation(np.resize(levels, k // 32))).repeat(32)
    a = np.empty((k // 512, 16))
    for p in range(k // 512):
        a[p, :8] = np.random.permutation(np.resize(levels, 8))
        for g in range(8):
            far = levels[np.abs(levels - a[p, g]) >= 10]
            a[p, g + 8] = far[np.random.randint(len(far))]
    return np.exp2(a.ravel()).repeat(32)


def f64(x):
    return np.asarray(x).astype(np.float64)


def striped(idx):
    return np.tile(np.asarray(idx).reshape(-1, 16).T, (8, 1)).astype(np.uint16)


def unstriped(offs):
    return offs[:16].T.reshape(-1).astype(np.int64)


def striped8(idx):
    return np.asarray(idx).reshape(8, -1, 16).transpose(0, 2, 1).reshape(128, -1).astype(np.uint16)


def unstriped8(offs):
    return offs.reshape(8, 16, -1).transpose(0, 2, 1).reshape(8, -1).astype(np.int64)


def pick8(x, idx, run):
    r = np.arange(len(x))
    return x[r[:, None], idx[r % (8 * run) // run]]


E2M1 = np.array([0.0, 0.5, 1.0, 1.5, 2.0, 3.0, 4.0, 6.0, -0.0, -0.5, -1.0, -1.5, -2.0, -3.0, -4.0, -6.0])


def pack_weight(w, fmt):
    k, n = w.shape
    w = f64(np.asarray(w, np.float32).astype(ml_dtypes.bfloat16)).reshape(k // 32, 32, n)
    amax = np.abs(w).max(1)
    if fmt in ("e4m3", "e5m2"):
        byte = np.frexp(amax)[1] - 1 + 127 - (7 if fmt == "e4m3" else 14)
    else:
        mant, ex = np.frexp(amax / 6.0)
        byte = np.where(mant > 0.5, ex, ex - 1) + 127
    byte = np.clip(np.where(amax > 0, byte, 1), 1, 254)
    scaled = (w * np.exp2(127.0 - byte)[:, None, :]).reshape(k, n).astype(np.float32)
    by_word = np.ascontiguousarray(scaled.reshape(k // 512, 128, 4, n).transpose(0, 1, 3, 2))
    if fmt in ("e4m3", "e5m2"):
        words = by_word.astype(ml_dtypes.float8_e4m3fn if fmt == "e4m3" else ml_dtypes.float8_e5m2).view(np.uint8)
    else:
        c = by_word.astype(ml_dtypes.float4_e2m1fn).view(np.uint8) & 0xF
        words = (c[..., 0::2] | (c[..., 1::2] << 4)).reshape(k // 512, 128, 2 * n)
    return np.ascontiguousarray(words), np.ascontiguousarray(byte.astype(np.uint8).reshape(k // 512, 16, n))


def unpack_weight(words, scales, fmt):
    g, _, n = scales.shape
    words = np.ascontiguousarray(words).reshape(g, 128, n, -1)
    if fmt in ("e4m3", "e5m2"):
        vals = words.view(ml_dtypes.float8_e4m3fn if fmt == "e4m3" else ml_dtypes.float8_e5m2).astype(np.float64)
    else:
        nib = np.empty((g, 128, n, 4), np.uint8)
        nib[..., 0::2] = words & 0xF
        nib[..., 1::2] = words >> 4
        vals = E2M1[nib]
    vals = vals * np.repeat(np.exp2(scales.astype(np.float64) - 127.0), 8, axis=1)[..., None]
    return vals.transpose(0, 1, 3, 2).reshape(g * 512, n)


K, T, J, R, C, O, N, S, E = 512, 1024, 256, 512, 512, 128, 256, 1024, 512


def setup_inputs():
    n = np.random.standard_normal
    idx = np.random.permutation(T)[:J]
    idx2 = np.stack([np.random.permutation(C)[:J] for _ in range(8)])
    idx3 = np.stack([np.random.permutation(C)[:O] for _ in range(8)])
    idx4 = np.stack([np.random.permutation(C)[:O] for _ in range(8)])
    idx5 = np.random.permutation(S)[:N]
    idx6 = np.stack([np.random.permutation(E)[:O] for _ in range(8)])
    idx7 = np.random.permutation(E)[:O]
    fk = mx_kscale(K)
    fr = mx_kscale(R)
    xtp = pack_weight(n((K, T)) / fk[:, None], "e2m1")
    wp = pack_weight(n((K, R)) * 1 / np.sqrt(K) * fk[:, None] * fr, "e5m2")
    vsp = pack_weight(n((R, S)) * 1 / np.sqrt(R) / fr[:, None], "e4m3")
    return {
        "xt_words": xtp[0],
        "xt_scales": xtp[1],
        "w_words": wp[0],
        "w_scales": wp[1],
        "sa": (np.random.uniform(0.5, 1.6, (R, 1))).astype(np.float32),
        "sb": (np.random.uniform(0.5, 1.6, (R, 1))).astype(np.float32),
        "vs_words": vsp[0],
        "vs_scales": vsp[1],
        "offs": striped(idx),
        "offs2": striped8(idx2),
        "offs3": striped8(idx3),
        "offs4": striped8(idx4),
        "offs5": striped(idx5),
        "offs6": striped8(idx6),
        "offs7": striped(idx7),
    }


def reference(xt_words, xt_scales, w_words, w_scales, sa, sb, vs_words, vs_scales, offs, offs2, offs3, offs4, offs5, offs6, offs7):
    idx = unstriped(offs)
    idx2 = unstriped8(offs2)
    idx3 = unstriped8(offs3)
    idx4 = unstriped8(offs4)
    idx5 = unstriped(offs5)
    idx6 = unstriped8(offs6)
    idx7 = unstriped(offs7)
    xtu = unpack_weight(xt_words, xt_scales, "e2m1")
    wu = unpack_weight(w_words, w_scales, "e5m2")
    vsu = unpack_weight(vs_words, vs_scales, "e4m3")
    xtidxg = xtu[:, idx]
    a = wu.T @ xtidxg
    pw = np.zeros((R, C))
    pw[np.arange(R)[:, None], idx2[np.arange(R) % 512 // 64]] = a
    hid = np.abs(pick8(pw, idx3, 64) * f64(sa) - pick8(pw, idx4, 64) * f64(sb))
    vsidx5g = vsu[:, idx5]
    hidq = mxq(hid, 0, "e5m2")
    p = vsidx5g.T @ hidq
    pa = np.zeros((N, E))
    pa[np.arange(N)[:, None], idx6[np.arange(N) % 128 // 16]] = p
    pb = np.zeros((N, E))
    pb[:, idx7] = p
    y = pa + pb
    return y

@@ -1,0 +1,172 @@
+from contextlib import ExitStack
+
+import concourse.mybir as mybir
+
+K, T, J, R, C, O, N, S, E = 512, 1024, 256, 512, 512, 128, 256, 1024, 512
+FLOPS = 2 * K * R * J + 2 * R * N * O
+
+F32 = mybir.dt.float32
+BF16 = mybir.dt.bfloat16
+I32 = mybir.dt.int32
+U32 = mybir.dt.uint32
+U16 = mybir.dt.uint16
+U8 = mybir.dt.uint8
+E2M1 = mybir.dt.float4_e2m1fn_x4
+E5M2 = mybir.dt.float8_e5m2_x4
+E4M3 = mybir.dt.float8_e4m3fn_x4
+COPY = mybir.ActivationFunctionType.Copy
+ALU = mybir.AluOpType
+
+P = 128
+PACK = 4
+QUADS = 4
+HALF = J // 2
+
+
+def tile_list_ownreads_solo_store_owntwopages_kernel(
+    tc, xt_words, xt_scales, w_words, w_scales, sa, sb, vs_words, vs_scales,
+    offs, offs2, offs3, offs4, offs5, offs6, offs7, out,
+):
+    nc = tc.nc
+    with ExitStack() as ctx:
+        lists = ctx.enter_context(tc.tile_pool(name="lists", bufs=1))
+        keep = ctx.enter_context(tc.tile_pool(name="keep", bufs=1))
+        psum = ctx.enter_context(tc.psum_pool(name="psum", bufs=1))
+
+        def load_list(name, src):
+            tile = lists.tile(list(src.shape), U16, name=name)
+            nc.sync.dma_start(tile[:], src)
+            return tile
+
+        def load_scale_rows(queue, plane, src, q):
+            queue.dma_start(plane[32 * q : 32 * q + 4, :].bitcast(I32), src[0, 4 * q : 4 * q + 4, :].bitcast(I32))
+
+        xs = keep.tile([P, T], U8, name="xs", tag="xs", align_bytes=64)
+        nc.vector.memset(xs[:].bitcast(I32), 0)
+        ws = keep.tile([P, R], U8, name="ws", tag="ws", align_bytes=64)
+        nc.vector.memset(ws[:].bitcast(I32), 0)
+
+        tok = load_list("tok", offs)
+        ws_rows = keep.tile([4, QUADS, R // 4], I32, name="ws_rows")
+        nc.scalar.dma_start(ws_rows[:], w_scales[0].bitcast(I32).rearrange("(q r) c -> r q c", r=4))
+        xw = keep.tile([P, T], U16, name="xw", tag="first_page", align_bytes=64)
+        nc.sync.dma_start(xw[:].bitcast(I32), xt_words[0].bitcast(I32))
+        ww = keep.tile([P, R], I32, name="ww", tag="second_page", align_bytes=64)
+        nc.scalar.dma_start(ww[:], w_words[0].rearrange("p c t -> p (c t)").bitcast(I32))
+        for q in range(QUADS):
+            load_scale_rows(nc.sync if q % 2 == 0 else nc.scalar, xs, xt_scales, q)
+        put = load_list("put", offs2)
+        pick_a = load_list("pick_a", offs3)
+        pick_b = load_list("pick_b", offs4)
+        sa_t = keep.tile([P, PACK], F32, name="sa_t")
+        nc.sync.dma_start(sa_t[:], sa.rearrange("(p t) o -> p (t o)", t=PACK))
+        sb_t = keep.tile([P, PACK], F32, name="sb_t")
+        nc.sync.dma_start(sb_t[:], sb.rearrange("(p t) o -> p (t o)", t=PACK))
+        vw = keep.tile([P, S], U32, name="vw", tag="vw", align_bytes=64)
+        nc.sync.dma_start(vw[:].bitcast(I32), vs_words[0].rearrange("p c t -> p (c t)").bitcast(I32))
+        entry = load_list("entry", offs5)
+        vsc = keep.tile([P, S], U8, name="vsc", tag="vsc", align_bytes=64)
+        nc.vector.memset(vsc[:].bitcast(I32), 0)
+        for q in range(QUADS):
+            load_scale_rows(nc.sync, vsc, vs_scales, q)
+        own = load_list("own", offs6)
+        common = load_list("common", offs7)
+
+        for q in range(QUADS):
+            nc.vector.tensor_copy(ws[32 * q : 32 * q + 4, :].bitcast(I32), ws_rows[:, q, :])
+
+        def deal(t, wd, sd):
+            nc.vector.tensor_copy(sd, ws[:, t:R:PACK])
+            nc.vector.tensor_copy(wd, ww[:, t:R:PACK])
+            return wd, sd
+
+        xg = keep.tile([P, J], U16, name="xg", align_bytes=64)
+        xsg = keep.tile([P, J], U8, name="xsg", align_bytes=64)
+
+        def gather_tokens(lo, hi):
+            part = tok[:, lo // 16 : hi // 16]
+            nc.vector.tensor_copy(xg[:, lo:hi], xw[:].indirect(part))
+            nc.vector.tensor_copy(xsg[:, lo:hi], xs[:].indirect(part))
+
+        def first_product(t, w_t, lo, hi, on_scalar):
+            acc = psum.tile([P, hi - lo], F32, name=f"a_ps{t}_{lo}")
+            nc.tensor.matmul_mx(
+                out=acc[:], lhsT=w_t[0].bitcast(E5M2), lhsT_scale=w_t[1],
+                rhs=xg[:, lo:hi].bitcast(E2M1), rhs_scale=xsg[:, lo:hi], start=True, stop=True,
+            )
+            a = keep.tile([P, hi - lo], F32, name=f"a{t}_{lo}")
+            if on_scalar:
+                nc.scalar.activation(a[:], acc[:], COPY)
+            else:
+                nc.vector.tensor_copy(a[:], acc[:])
+            return a
+
+        def new_page(name, tag):
+            page = keep.tile([P, C], F32, name=name, tag=tag, align_bytes=64)
+            nc.gpsimd.memset(page[:], 0.0)
+            return page
+
+        boards = [new_page(f"board{t}", f"board{t}") for t in range(PACK)]
+
+        def put_on_board(t, a, lo, hi):
+            nc.scalar.activation(boards[t][:].indirect(put[:, lo // 16 : hi // 16]), a[:], COPY)
+
+        def read_board(t, diff):
+            ga = keep.tile([P, O], F32, name=f"ga{t}")
+            nc.scalar.activation(ga[:], boards[t][:].indirect(pick_a[:]), COPY, scale=sa_t[:, t : t + 1])
+            gb = keep.tile([P, O], F32, name=f"gb{t}")
+            nc.scalar.activation(gb[:], boards[t][:].indirect(pick_b[:]), COPY, scale=sb_t[:, t : t + 1])
+            nc.vector.tensor_tensor(diff, ga[:], gb[:], ALU.subtract)
+
+        wd0 = keep.tile([P, P], I32, name="wd0", align_bytes=64)
+        sd0 = keep.tile([P, P], U8, name="sd0", align_bytes=64)
+        w0 = deal(0, wd0[:], sd0[:])
+        gather_tokens(0, HALF)
+        put_on_board(0, first_product(0, w0, 0, HALF, True), 0, HALF)
+        gather_tokens(HALF, J)
+        put_on_board(0, first_product(0, w0, HALF, J, False), HALF, J)
+        wd_rest = keep.tile([P, (PACK - 1) * P], I32, name="wd_rest", tag="first_page", align_bytes=64)
+        sd_rest = keep.tile([P, (PACK - 1) * P], U8, name="sd_rest", tag="xs", align_bytes=64)
+        for t in range(1, PACK):
+            cols = slice((t - 1) * P, t * P)
+            put_on_board(t, first_product(t, deal(t, wd_rest[:, cols], sd_rest[:, cols]), 0, J, False), 0, J)
+
+        vg = keep.tile([P, N], U32, name="vg", align_bytes=64)
+        nc.vector.tensor_copy(vg[:], vw[:].indirect(entry[:]))
+        vsg = keep.tile([P, N], U8, name="vsg", align_bytes=64)
+        nc.vector.tensor_copy(vsg[:], vsc[:].indirect(entry[:]))
+        pa = [new_page("pa0", "first_page"), new_page("pa1", "second_page")]
+        pb = [new_page("pb0", "xs"), new_page("pb1", "ws")]
+
+        diff = keep.tile([P, PACK, O], F32, name="diff", tag="vw", align_bytes=64)
+        hid = keep.tile([P, O, PACK], BF16, name="hid", tag="vsc", align_bytes=64)
+        for t0 in range(0, PACK, 2):
+            read_board(t0, diff[:, t0, :])
+            read_board(t0 + 1, diff[:, t0 + 1, :])
+            pair = diff[:, t0 : t0 + 2, :].rearrange("p t o -> p o t")
+            nc.vector.scalar_tensor_tensor(hid[:, :, t0 : t0 + 2], pair, -1.0, pair, ALU.mult, ALU.max)
+
+        hq = keep.tile([P, O], U32, name="hq", align_bytes=64)
+        hs = keep.tile([P, O], U8, name="hs", align_bytes=64)
+        nc.vector.quantize_mx(out=hq[:].bitcast(E5M2), scales=hs[:], in_=hid[:].rearrange("p o t -> p (o t)"))
+
+        prods = []
+        for m in range(N // P):
+            cols = slice(m * P, (m + 1) * P)
+            acc = psum.tile([P, O], F32, name=f"p_ps{m}")
+            nc.tensor.matmul_mx(
+                out=acc[:], lhsT=vg[:, cols].bitcast(E4M3), lhsT_scale=vsg[:, cols],
+                rhs=hq[:].bitcast(E5M2), rhs_scale=hs[:], start=True, stop=True,
+            )
+            prod = keep.tile([P, O], F32, name=f"prod{m}")
+            if m == 0:
+                nc.scalar.activation(prod[:], acc[:], COPY)
+            else:
+                nc.vector.tensor_copy(prod[:], acc[:])
+            prods.append(prod)
+        for m in range(N // P):
+            nc.scalar.activation(pa[m][:].indirect(own[:]), prods[m][:], COPY)
+            nc.vector.tensor_copy(pb[m][:].indirect(common[:]), prods[m][:])
+            y = keep.tile([P, E], F32, name=f"y{m}")
+            nc.vector.tensor_tensor(y[:], pa[m][:], pb[m][:], ALU.add)
+            nc.sync.dma_start(out[m * P : (m + 1) * P, :], y[:])

@@ -15,6 +15,7 @@ E2M1 = mybir.dt.float4_e2m1fn_x4
 E5M2 = mybir.dt.float8_e5m2_x4
 E4M3 = mybir.dt.float8_e4m3fn_x4
 COPY = mybir.ActivationFunctionType.Copy
+ABS = mybir.ActivationFunctionType.Abs
 ALU = mybir.AluOpType
 
 P = 128
@@ -51,10 +52,14 @@ def tile_list_ownreads_solo_store_owntwopages_kernel(
         nc.scalar.dma_start(ws_rows[:], w_scales[0].bitcast(I32).rearrange("(q r) c -> r q c", r=4))
         xw = keep.tile([P, T], U16, name="xw", tag="first_page", align_bytes=64)
         nc.sync.dma_start(xw[:].bitcast(I32), xt_words[0].bitcast(I32))
-        ww = keep.tile([P, R], I32, name="ww", tag="second_page", align_bytes=64)
-        nc.scalar.dma_start(ww[:], w_words[0].rearrange("p c t -> p (c t)").bitcast(I32))
         for q in range(QUADS):
-            load_scale_rows(nc.sync if q % 2 == 0 else nc.scalar, xs, xt_scales, q)
+            load_scale_rows(nc.sync if q < QUADS // 2 else nc.scalar, xs, xt_scales, q)
+        ww = keep.tile([P, R], U32, name="ww", tag="second_page", align_bytes=64)
+        nc.scalar.dma_start(ww[:].bitcast(I32), w_words[0].rearrange("p c t -> p (c t)").bitcast(I32))
+        warm_in = keep.tile([P, 1], F32, name="warm_in")
+        nc.gpsimd.memset(warm_in[:], 0.0)
+        warm_out = keep.tile([P, 1], F32, name="warm_out")
+        nc.scalar.activation(warm_out[:], warm_in[:], COPY)
         put = load_list("put", offs2)
         pick_a = load_list("pick_a", offs3)
         pick_b = load_list("pick_b", offs4)
@@ -75,18 +80,22 @@ def tile_list_ownreads_solo_store_owntwopages_kernel(
         for q in range(QUADS):
             nc.vector.tensor_copy(ws[32 * q : 32 * q + 4, :].bitcast(I32), ws_rows[:, q, :])
 
-        def deal(t, wd, sd):
+        def deal_words(t):
+            wd = keep.tile([P, P], U32, name=f"wd{t}", align_bytes=64)
+            nc.scalar.copy(wd[:], ww[:, t:R:PACK])
+            return wd[:]
+
+        def deal_scales(t, sd):
             nc.vector.tensor_copy(sd, ws[:, t:R:PACK])
-            nc.vector.tensor_copy(wd, ww[:, t:R:PACK])
-            return wd, sd
+            return sd
 
         xg = keep.tile([P, J], U16, name="xg", align_bytes=64)
         xsg = keep.tile([P, J], U8, name="xsg", align_bytes=64)
 
         def gather_tokens(lo, hi):
             part = tok[:, lo // 16 : hi // 16]
-            nc.vector.tensor_copy(xg[:, lo:hi], xw[:].indirect(part))
             nc.vector.tensor_copy(xsg[:, lo:hi], xs[:].indirect(part))
+            nc.vector.tensor_copy(xg[:, lo:hi], xw[:].indirect(part))
 
         def first_product(t, w_t, lo, hi, on_scalar):
             acc = psum.tile([P, hi - lo], F32, name=f"a_ps{t}_{lo}")
@@ -101,50 +110,61 @@ def tile_list_ownreads_solo_store_owntwopages_kernel(
                 nc.vector.tensor_copy(a[:], acc[:])
             return a
 
-        def new_page(name, tag):
+        def new_page(name, tag, engine):
             page = keep.tile([P, C], F32, name=name, tag=tag, align_bytes=64)
-            nc.gpsimd.memset(page[:], 0.0)
+            engine.memset(page[:], 0.0)
             return page
 
-        boards = [new_page(f"board{t}", f"board{t}") for t in range(PACK)]
+        boards = [new_page(f"board{t}", f"board{t}", nc.vector) for t in range(PACK)]
 
         def put_on_board(t, a, lo, hi):
             nc.scalar.activation(boards[t][:].indirect(put[:, lo // 16 : hi // 16]), a[:], COPY)
 
-        def read_board(t, diff):
+        def read_board(t):
             ga = keep.tile([P, O], F32, name=f"ga{t}")
             nc.scalar.activation(ga[:], boards[t][:].indirect(pick_a[:]), COPY, scale=sa_t[:, t : t + 1])
             gb = keep.tile([P, O], F32, name=f"gb{t}")
             nc.scalar.activation(gb[:], boards[t][:].indirect(pick_b[:]), COPY, scale=sb_t[:, t : t + 1])
-            nc.vector.tensor_tensor(diff, ga[:], gb[:], ALU.subtract)
+            return ga, gb
 
-        wd0 = keep.tile([P, P], I32, name="wd0", align_bytes=64)
+        wd = [deal_words(t) for t in range(PACK)]
         sd0 = keep.tile([P, P], U8, name="sd0", align_bytes=64)
-        w0 = deal(0, wd0[:], sd0[:])
+        w0 = (wd[0], deal_scales(0, sd0[:]))
         gather_tokens(0, HALF)
         put_on_board(0, first_product(0, w0, 0, HALF, True), 0, HALF)
         gather_tokens(HALF, J)
         put_on_board(0, first_product(0, w0, HALF, J, False), HALF, J)
-        wd_rest = keep.tile([P, (PACK - 1) * P], I32, name="wd_rest", tag="first_page", align_bytes=64)
         sd_rest = keep.tile([P, (PACK - 1) * P], U8, name="sd_rest", tag="xs", align_bytes=64)
         for t in range(1, PACK):
             cols = slice((t - 1) * P, t * P)
-            put_on_board(t, first_product(t, deal(t, wd_rest[:, cols], sd_rest[:, cols]), 0, J, False), 0, J)
+            put_on_board(t, first_product(t, (wd[t], deal_scales(t, sd_rest[:, cols])), 0, J, False), 0, J)
 
         vg = keep.tile([P, N], U32, name="vg", align_bytes=64)
         nc.vector.tensor_copy(vg[:], vw[:].indirect(entry[:]))
         vsg = keep.tile([P, N], U8, name="vsg", align_bytes=64)
         nc.vector.tensor_copy(vsg[:], vsc[:].indirect(entry[:]))
-        pa = [new_page("pa0", "first_page"), new_page("pa1", "second_page")]
-        pb = [new_page("pb0", "xs"), new_page("pb1", "ws")]
+        pa = [new_page("pa0", "first_page", nc.gpsimd), new_page("pa1", "second_page", nc.gpsimd)]
+        pb = [new_page("pb0", "xs", nc.gpsimd), new_page("pb1", "ws", nc.gpsimd)]
 
         diff = keep.tile([P, PACK, O], F32, name="diff", tag="vw", align_bytes=64)
         hid = keep.tile([P, O, PACK], BF16, name="hid", tag="vsc", align_bytes=64)
-        for t0 in range(0, PACK, 2):
-            read_board(t0, diff[:, t0, :])
-            read_board(t0 + 1, diff[:, t0 + 1, :])
-            pair = diff[:, t0 : t0 + 2, :].rearrange("p t o -> p o t")
-            nc.vector.scalar_tensor_tensor(hid[:, :, t0 : t0 + 2], pair, -1.0, pair, ALU.mult, ALU.max)
+
+        def pair_of(t0, cols):
+            return diff[:, t0 : t0 + 2, cols].rearrange("p t o -> p o t")
+
+        def magnitude_on_vector(t0, cols):
+            pair = pair_of(t0, cols)
+            nc.vector.scalar_tensor_tensor(hid[:, cols, t0 : t0 + 2], pair, -1.0, pair, ALU.mult, ALU.max)
+
+        low, high, whole = slice(0, O // 2), slice(O // 2, O), slice(0, O)
+        for t in range(PACK):
+            ga, gb = read_board(t)
+            for cols in (low, high) if t == PACK - 1 else (whole,):
+                nc.vector.tensor_tensor(diff[:, t, cols], ga[:, cols], gb[:, cols], ALU.subtract)
+            if t == 1:
+                magnitude_on_vector(0, whole)
+        magnitude_on_vector(2, low)
+        nc.scalar.activation(hid[:, high, 2:4], pair_of(2, high), ABS)
 
         hq = keep.tile([P, O], U32, name="hq", align_bytes=64)
         hs = keep.tile([P, O], U8, name="hs", align_bytes=64)
@@ -164,9 +184,18 @@ def tile_list_ownreads_solo_store_owntwopages_kernel(
             else:
                 nc.vector.tensor_copy(prod[:], acc[:])
             prods.append(prod)
-        for m in range(N // P):
-            nc.scalar.activation(pa[m][:].indirect(own[:]), prods[m][:], COPY)
-            nc.vector.tensor_copy(pb[m][:].indirect(common[:]), prods[m][:])
-            y = keep.tile([P, E], F32, name=f"y{m}")
-            nc.vector.tensor_tensor(y[:], pa[m][:], pb[m][:], ALU.add)
-            nc.sync.dma_start(out[m * P : (m + 1) * P, :], y[:])
+        half_list = O // 32
+        nc.scalar.activation(pa[0][:].indirect(own[:]), prods[0][:], COPY)
+        nc.vector.tensor_copy(pb[0][:].indirect(common[:]), prods[0][:])
+        nc.scalar.activation(pa[1][:].indirect(own[:]), prods[1][:], COPY)
+        nc.vector.tensor_copy(pb[1][:].indirect(common[:, :half_list]), prods[1][:, low])
+        nc.scalar.activation(pb[1][:].indirect(common[:, half_list:]), prods[1][:, high], COPY)
+
+        def add_and_store(m, cols, queue):
+            y = keep.tile([P, cols.stop - cols.start], F32, name=f"y{m}_{cols.start}")
+            nc.vector.tensor_tensor(y[:], pa[m][:, cols], pb[m][:, cols], ALU.add)
+            queue.dma_start(out[m * P : (m + 1) * P, cols], y[:])
+
+        add_and_store(0, slice(0, E), nc.sync)
+        add_and_store(1, slice(0, E // 2), nc.sync)
+        add_and_store(1, slice(E // 2, E), nc.scalar)

@@ -49,15 +49,15 @@ def tile_list_ownreads_solo_store_owntwopages_kernel(
 
         tok = load_list("tok", offs)
         ws_rows = keep.tile([4, QUADS, R // 4], I32, name="ws_rows")
-        nc.scalar.dma_start(ws_rows[:], w_scales[0].bitcast(I32).rearrange("(q r) c -> r q c", r=4))
-        xw = keep.tile([P, T], U16, name="xw", tag="first_page", align_bytes=64)
+        nc.sync.dma_start(ws_rows[:], w_scales[0].bitcast(I32).rearrange("(q r) c -> r q c", r=4))
+        xw = keep.tile([P, T], U16, name="xw", align_bytes=64)
         nc.sync.dma_start(xw[:].bitcast(I32), xt_words[0].bitcast(I32))
         for q in range(QUADS):
-            load_scale_rows(nc.sync if q < QUADS // 2 else nc.scalar, xs, xt_scales, q)
-        ww = keep.tile([P, R], U32, name="ww", tag="second_page", align_bytes=64)
-        nc.scalar.dma_start(ww[:].bitcast(I32), w_words[0].rearrange("p c t -> p (c t)").bitcast(I32))
+            load_scale_rows(nc.scalar, xs, xt_scales, q)
+        ww = keep.tile([P, R], U32, name="ww", align_bytes=64)
+        nc.sync.dma_start(ww[:].bitcast(I32), w_words[0].rearrange("p c t -> p (c t)").bitcast(I32))
         warm_in = keep.tile([P, 1], F32, name="warm_in")
-        nc.gpsimd.memset(warm_in[:], 0.0)
+        nc.vector.memset(warm_in[:], 0.0)
         warm_out = keep.tile([P, 1], F32, name="warm_out")
         nc.scalar.activation(warm_out[:], warm_in[:], COPY)
         put = load_list("put", offs2)
@@ -80,11 +80,6 @@ def tile_list_ownreads_solo_store_owntwopages_kernel(
         for q in range(QUADS):
             nc.vector.tensor_copy(ws[32 * q : 32 * q + 4, :].bitcast(I32), ws_rows[:, q, :])
 
-        def deal_words(t):
-            wd = keep.tile([P, P], U32, name=f"wd{t}", align_bytes=64)
-            nc.scalar.copy(wd[:], ww[:, t:R:PACK])
-            return wd[:]
-
         def deal_scales(t, sd):
             nc.vector.tensor_copy(sd, ws[:, t:R:PACK])
             return sd
@@ -103,7 +98,7 @@ def tile_list_ownreads_solo_store_owntwopages_kernel(
                 out=acc[:], lhsT=w_t[0].bitcast(E5M2), lhsT_scale=w_t[1],
                 rhs=xg[:, lo:hi].bitcast(E2M1), rhs_scale=xsg[:, lo:hi], start=True, stop=True,
             )
-            a = keep.tile([P, hi - lo], F32, name=f"a{t}_{lo}")
+            a = keep.tile([P, hi - lo], F32, name=f"a{t}_{lo}", tag=f"a{t}_{lo}", align_bytes=64)
             if on_scalar:
                 nc.scalar.activation(a[:], acc[:], COPY)
             else:
@@ -115,7 +110,7 @@ def tile_list_ownreads_solo_store_owntwopages_kernel(
             engine.memset(page[:], 0.0)
             return page
 
-        boards = [new_page(f"board{t}", f"board{t}", nc.vector) for t in range(PACK)]
+        boards = [new_page(f"board{t}", f"board{t}", nc.vector) for t in range(2)]
 
         def put_on_board(t, a, lo, hi):
             nc.scalar.activation(boards[t][:].indirect(put[:, lo // 16 : hi // 16]), a[:], COPY)
@@ -127,24 +122,42 @@ def tile_list_ownreads_solo_store_owntwopages_kernel(
             nc.scalar.activation(gb[:], boards[t][:].indirect(pick_b[:]), COPY, scale=sb_t[:, t : t + 1])
             return ga, gb
 
-        wd = [deal_words(t) for t in range(PACK)]
-        sd0 = keep.tile([P, P], U8, name="sd0", align_bytes=64)
-        w0 = (wd[0], deal_scales(0, sd0[:]))
+        wd0 = keep.tile([P, P], U32, name="wd0", align_bytes=64)
+        nc.scalar.copy(wd0[:], ww[:, 0:R:PACK])
+        wd_rest = keep.tile([P, PACK - 1, P], U32, name="wd_rest", align_bytes=64)
+        nc.scalar.copy(
+            wd_rest[:].rearrange("p t m -> p m t"),
+            ww[:].rearrange("p (m t) -> p m t", t=PACK)[:, :, 1:PACK],
+        )
+        wd = [wd0[:]] + [wd_rest[:, t, :] for t in range(PACK - 1)]
+        sd = []
+        for t in range(2):
+            sd_t = keep.tile([P, P], U8, name=f"sd{t}", align_bytes=64)
+            sd.append(sd_t[:])
+        deal_scales(0, sd[0])
         gather_tokens(0, HALF)
-        put_on_board(0, first_product(0, w0, 0, HALF, True), 0, HALF)
+        put_on_board(0, first_product(0, (wd[0], sd[0]), 0, HALF, True), 0, HALF)
+        deal_scales(1, sd[1])
+        put_on_board(1, first_product(1, (wd[1], sd[1]), 0, HALF, False), 0, HALF)
         gather_tokens(HALF, J)
-        put_on_board(0, first_product(0, w0, HALF, J, False), HALF, J)
-        sd_rest = keep.tile([P, (PACK - 1) * P], U8, name="sd_rest", tag="xs", align_bytes=64)
-        for t in range(1, PACK):
-            cols = slice((t - 1) * P, t * P)
-            put_on_board(t, first_product(t, (wd[t], deal_scales(t, sd_rest[:, cols])), 0, J, False), 0, J)
+        for t in range(2):
+            put_on_board(t, first_product(t, (wd[t], sd[t]), HALF, J, False), HALF, J)
+        sd_rest = keep.tile([P, 2 * P], U8, name="sd_rest", tag="xs", align_bytes=64)
+        rest = []
+        for t in range(2, PACK):
+            cols = slice((t - 2) * P, (t - 1) * P)
+            rest.append(first_product(t, (wd[t], deal_scales(t, sd_rest[:, cols])), 0, J, False))
+        boards.append(new_page("board2", "ws", nc.gpsimd))
+        boards.append(new_page("board3", "xs", nc.gpsimd))
+        for t in range(2, PACK):
+            put_on_board(t, rest[t - 2], 0, J)
 
         vg = keep.tile([P, N], U32, name="vg", align_bytes=64)
         nc.vector.tensor_copy(vg[:], vw[:].indirect(entry[:]))
         vsg = keep.tile([P, N], U8, name="vsg", align_bytes=64)
         nc.vector.tensor_copy(vsg[:], vsc[:].indirect(entry[:]))
-        pa = [new_page("pa0", "first_page", nc.gpsimd), new_page("pa1", "second_page", nc.gpsimd)]
-        pb = [new_page("pb0", "xs", nc.gpsimd), new_page("pb1", "ws", nc.gpsimd)]
+        pa = [new_page("pa0", "a0_0", nc.gpsimd), new_page("pa1", "a1_0", nc.gpsimd)]
+        pb = [new_page("pb0", f"a0_{HALF}", nc.gpsimd), new_page("pb1", f"a1_{HALF}", nc.gpsimd)]
 
         diff = keep.tile([P, PACK, O], F32, name="diff", tag="vw", align_bytes=64)
         hid = keep.tile([P, O, PACK], BF16, name="hid", tag="vsc", align_bytes=64)

@@ -49,13 +49,13 @@ def tile_list_ownreads_solo_store_owntwopages_kernel(
 
         tok = load_list("tok", offs)
         ws_rows = keep.tile([4, QUADS, R // 4], I32, name="ws_rows")
-        nc.sync.dma_start(ws_rows[:], w_scales[0].bitcast(I32).rearrange("(q r) c -> r q c", r=4))
+        nc.scalar.dma_start(ws_rows[:], w_scales[0].bitcast(I32).rearrange("(q r) c -> r q c", r=4))
         xw = keep.tile([P, T], U16, name="xw", align_bytes=64)
         nc.sync.dma_start(xw[:].bitcast(I32), xt_words[0].bitcast(I32))
         for q in range(QUADS):
-            load_scale_rows(nc.scalar, xs, xt_scales, q)
+            load_scale_rows(nc.sync if q < QUADS // 2 else nc.scalar, xs, xt_scales, q)
         ww = keep.tile([P, R], U32, name="ww", align_bytes=64)
-        nc.sync.dma_start(ww[:].bitcast(I32), w_words[0].rearrange("p c t -> p (c t)").bitcast(I32))
+        nc.scalar.dma_start(ww[:].bitcast(I32), w_words[0].rearrange("p c t -> p (c t)").bitcast(I32))
         warm_in = keep.tile([P, 1], F32, name="warm_in")
         nc.vector.memset(warm_in[:], 0.0)
         warm_out = keep.tile([P, 1], F32, name="warm_out")
@@ -156,8 +156,7 @@ def tile_list_ownreads_solo_store_owntwopages_kernel(
         nc.vector.tensor_copy(vg[:], vw[:].indirect(entry[:]))
         vsg = keep.tile([P, N], U8, name="vsg", align_bytes=64)
         nc.vector.tensor_copy(vsg[:], vsc[:].indirect(entry[:]))
-        pa = [new_page("pa0", "a0_0", nc.gpsimd), new_page("pa1", "a1_0", nc.gpsimd)]
-        pb = [new_page("pb0", f"a0_{HALF}", nc.gpsimd), new_page("pb1", f"a1_{HALF}", nc.gpsimd)]
+        pa = [new_page("pa0", "a2_0", nc.gpsimd), new_page("pa1", "a3_0", nc.gpsimd)]
 
         diff = keep.tile([P, PACK, O], F32, name="diff", tag="vw", align_bytes=64)
         hid = keep.tile([P, O, PACK], BF16, name="hid", tag="vsc", align_bytes=64)
@@ -176,6 +175,7 @@ def tile_list_ownreads_solo_store_owntwopages_kernel(
                 nc.vector.tensor_tensor(diff[:, t, cols], ga[:, cols], gb[:, cols], ALU.subtract)
             if t == 1:
                 magnitude_on_vector(0, whole)
+        pb = [new_page(f"pb{m}", f"board{m}", nc.gpsimd) for m in range(N // P)]
         magnitude_on_vector(2, low)
         nc.scalar.activation(hid[:, high, 2:4], pair_of(2, high), ABS)
 

@@ -56,10 +56,6 @@ def tile_list_ownreads_solo_store_owntwopages_kernel(
             load_scale_rows(nc.sync if q < QUADS // 2 else nc.scalar, xs, xt_scales, q)
         ww = keep.tile([P, R], U32, name="ww", align_bytes=64)
         nc.scalar.dma_start(ww[:].bitcast(I32), w_words[0].rearrange("p c t -> p (c t)").bitcast(I32))
-        warm_in = keep.tile([P, 1], F32, name="warm_in")
-        nc.vector.memset(warm_in[:], 0.0)
-        warm_out = keep.tile([P, 1], F32, name="warm_out")
-        nc.scalar.activation(warm_out[:], warm_in[:], COPY)
         put = load_list("put", offs2)
         pick_a = load_list("pick_a", offs3)
         pick_b = load_list("pick_b", offs4)

from contextlib import ExitStack

import concourse.mybir as mybir

K, T, J, R, C, O, N, S, E = 512, 1024, 256, 512, 512, 128, 256, 1024, 512
FLOPS = 2 * K * R * J + 2 * R * N * O

F32 = mybir.dt.float32
BF16 = mybir.dt.bfloat16
I32 = mybir.dt.int32
U32 = mybir.dt.uint32
U16 = mybir.dt.uint16
U8 = mybir.dt.uint8
E2M1 = mybir.dt.float4_e2m1fn_x4
E5M2 = mybir.dt.float8_e5m2_x4
E4M3 = mybir.dt.float8_e4m3fn_x4
COPY = mybir.ActivationFunctionType.Copy
ABS = mybir.ActivationFunctionType.Abs
ALU = mybir.AluOpType

P = 128
PACK = 4
QUADS = 4
HALF = J // 2


def tile_list_ownreads_solo_store_owntwopages_kernel(
    tc, xt_words, xt_scales, w_words, w_scales, sa, sb, vs_words, vs_scales,
    offs, offs2, offs3, offs4, offs5, offs6, offs7, out,
):
    nc = tc.nc
    with ExitStack() as ctx:
        lists = ctx.enter_context(tc.tile_pool(name="lists", bufs=1))
        keep = ctx.enter_context(tc.tile_pool(name="keep", bufs=1))
        psum = ctx.enter_context(tc.psum_pool(name="psum", bufs=1))

        def load_list(name, src):
            tile = lists.tile(list(src.shape), U16, name=name)
            nc.sync.dma_start(tile[:], src)
            return tile

        def load_scale_rows(queue, plane, src, q):
            queue.dma_start(plane[32 * q : 32 * q + 4, :].bitcast(I32), src[0, 4 * q : 4 * q + 4, :].bitcast(I32))

        xs = keep.tile([P, T], U8, name="xs", tag="xs", align_bytes=64)
        nc.vector.memset(xs[:].bitcast(I32), 0)
        ws = keep.tile([P, R], U8, name="ws", tag="ws", align_bytes=64)
        nc.vector.memset(ws[:].bitcast(I32), 0)

        tok = load_list("tok", offs)
        ws_rows = keep.tile([4, QUADS, R // 4], I32, name="ws_rows")
        nc.scalar.dma_start(ws_rows[:], w_scales[0].bitcast(I32).rearrange("(q r) c -> r q c", r=4))
        xw = keep.tile([P, T], U16, name="xw", align_bytes=64)
        nc.sync.dma_start(xw[:].bitcast(I32), xt_words[0].bitcast(I32))
        for q in range(QUADS):
            load_scale_rows(nc.sync if q < QUADS // 2 else nc.scalar, xs, xt_scales, q)
        ww = keep.tile([P, R], U32, name="ww", align_bytes=64)
        nc.scalar.dma_start(ww[:].bitcast(I32), w_words[0].rearrange("p c t -> p (c t)").bitcast(I32))
        put = load_list("put", offs2)
        pick_a = load_list("pick_a", offs3)
        pick_b = load_list("pick_b", offs4)
        sa_t = keep.tile([P, PACK], F32, name="sa_t")
        nc.sync.dma_start(sa_t[:], sa.rearrange("(p t) o -> p (t o)", t=PACK))
        sb_t = keep.tile([P, PACK], F32, name="sb_t")
        nc.sync.dma_start(sb_t[:], sb.rearrange("(p t) o -> p (t o)", t=PACK))
        vw = keep.tile([P, S], U32, name="vw", tag="vw", align_bytes=64)
        nc.sync.dma_start(vw[:].bitcast(I32), vs_words[0].rearrange("p c t -> p (c t)").bitcast(I32))
        entry = load_list("entry", offs5)
        vsc = keep.tile([P, S], U8, name="vsc", tag="vsc", align_bytes=64)
        nc.vector.memset(vsc[:].bitcast(I32), 0)
        for q in range(QUADS):
            load_scale_rows(nc.sync, vsc, vs_scales, q)
        own = load_list("own", offs6)
        common = load_list("common", offs7)

        for q in range(QUADS):
            nc.vector.tensor_copy(ws[32 * q : 32 * q + 4, :].bitcast(I32), ws_rows[:, q, :])

        def deal_scales(t, sd):
            nc.vector.tensor_copy(sd, ws[:, t:R:PACK])
            return sd

        xg = keep.tile([P, J], U16, name="xg", align_bytes=64)
        xsg = keep.tile([P, J], U8, name="xsg", align_bytes=64)

        def gather_tokens(lo, hi):
            part = tok[:, lo // 16 : hi // 16]
            nc.vector.tensor_copy(xsg[:, lo:hi], xs[:].indirect(part))
            nc.vector.tensor_copy(xg[:, lo:hi], xw[:].indirect(part))

        def first_product(t, w_t, lo, hi, on_scalar):
            acc = psum.tile([P, hi - lo], F32, name=f"a_ps{t}_{lo}")
            nc.tensor.matmul_mx(
                out=acc[:], lhsT=w_t[0].bitcast(E5M2), lhsT_scale=w_t[1],
                rhs=xg[:, lo:hi].bitcast(E2M1), rhs_scale=xsg[:, lo:hi], start=True, stop=True,
            )
            a = keep.tile([P, hi - lo], F32, name=f"a{t}_{lo}", tag=f"a{t}_{lo}", align_bytes=64)
            if on_scalar:
                nc.scalar.activation(a[:], acc[:], COPY)
            else:
                nc.vector.tensor_copy(a[:], acc[:])
            return a

        def new_page(name, tag, engine):
            page = keep.tile([P, C], F32, name=name, tag=tag, align_bytes=64)
            engine.memset(page[:], 0.0)
            return page

        boards = [new_page(f"board{t}", f"board{t}", nc.vector) for t in range(2)]

        def put_on_board(t, a, lo, hi):
            nc.scalar.activation(boards[t][:].indirect(put[:, lo // 16 : hi // 16]), a[:], COPY)

        def read_board(t):
            ga = keep.tile([P, O], F32, name=f"ga{t}")
            nc.scalar.activation(ga[:], boards[t][:].indirect(pick_a[:]), COPY, scale=sa_t[:, t : t + 1])
            gb = keep.tile([P, O], F32, name=f"gb{t}")
            nc.scalar.activation(gb[:], boards[t][:].indirect(pick_b[:]), COPY, scale=sb_t[:, t : t + 1])
            return ga, gb

        wd0 = keep.tile([P, P], U32, name="wd0", align_bytes=64)
        nc.scalar.copy(wd0[:], ww[:, 0:R:PACK])
        wd_rest = keep.tile([P, PACK - 1, P], U32, name="wd_rest", align_bytes=64)
        nc.scalar.copy(
            wd_rest[:].rearrange("p t m -> p m t"),
            ww[:].rearrange("p (m t) -> p m t", t=PACK)[:, :, 1:PACK],
        )
        wd = [wd0[:]] + [wd_rest[:, t, :] for t in range(PACK - 1)]
        sd = []
        for t in range(2):
            sd_t = keep.tile([P, P], U8, name=f"sd{t}", align_bytes=64)
            sd.append(sd_t[:])
        deal_scales(0, sd[0])
        gather_tokens(0, HALF)
        put_on_board(0, first_product(0, (wd[0], sd[0]), 0, HALF, True), 0, HALF)
        deal_scales(1, sd[1])
        put_on_board(1, first_product(1, (wd[1], sd[1]), 0, HALF, False), 0, HALF)
        gather_tokens(HALF, J)
        for t in range(2):
            put_on_board(t, first_product(t, (wd[t], sd[t]), HALF, J, False), HALF, J)
        sd_rest = keep.tile([P, 2 * P], U8, name="sd_rest", tag="xs", align_bytes=64)
        rest = []
        for t in range(2, PACK):
            cols = slice((t - 2) * P, (t - 1) * P)
            rest.append(first_product(t, (wd[t], deal_scales(t, sd_rest[:, cols])), 0, J, False))
        boards.append(new_page("board2", "ws", nc.gpsimd))
        boards.append(new_page("board3", "xs", nc.gpsimd))
        for t in range(2, PACK):
            put_on_board(t, rest[t - 2], 0, J)

        vg = keep.tile([P, N], U32, name="vg", align_bytes=64)
        nc.vector.tensor_copy(vg[:], vw[:].indirect(entry[:]))
        vsg = keep.tile([P, N], U8, name="vsg", align_bytes=64)
        nc.vector.tensor_copy(vsg[:], vsc[:].indirect(entry[:]))
        pa = [new_page("pa0", "a2_0", nc.gpsimd), new_page("pa1", "a3_0", nc.gpsimd)]

        diff = keep.tile([P, PACK, O], F32, name="diff", tag="vw", align_bytes=64)
        hid = keep.tile([P, O, PACK], BF16, name="hid", tag="vsc", align_bytes=64)

        def pair_of(t0, cols):
            return diff[:, t0 : t0 + 2, cols].rearrange("p t o -> p o t")

        def magnitude_on_vector(t0, cols):
            pair = pair_of(t0, cols)
            nc.vector.scalar_tensor_tensor(hid[:, cols, t0 : t0 + 2], pair, -1.0, pair, ALU.mult, ALU.max)

        low, high, whole = slice(0, O // 2), slice(O // 2, O), slice(0, O)
        for t in range(PACK):
            ga, gb = read_board(t)
            for cols in (low, high) if t == PACK - 1 else (whole,):
                nc.vector.tensor_tensor(diff[:, t, cols], ga[:, cols], gb[:, cols], ALU.subtract)
            if t == 1:
                magnitude_on_vector(0, whole)
        pb = [new_page(f"pb{m}", f"board{m}", nc.gpsimd) for m in range(N // P)]
        magnitude_on_vector(2, low)
        nc.scalar.activation(hid[:, high, 2:4], pair_of(2, high), ABS)

        hq = keep.tile([P, O], U32, name="hq", align_bytes=64)
        hs = keep.tile([P, O], U8, name="hs", align_bytes=64)
        nc.vector.quantize_mx(out=hq[:].bitcast(E5M2), scales=hs[:], in_=hid[:].rearrange("p o t -> p (o t)"))

        prods = []
        for m in range(N // P):
            cols = slice(m * P, (m + 1) * P)
            acc = psum.tile([P, O], F32, name=f"p_ps{m}")
            nc.tensor.matmul_mx(
                out=acc[:], lhsT=vg[:, cols].bitcast(E4M3), lhsT_scale=vsg[:, cols],
                rhs=hq[:].bitcast(E5M2), rhs_scale=hs[:], start=True, stop=True,
            )
            prod = keep.tile([P, O], F32, name=f"prod{m}")
            if m == 0:
                nc.scalar.activation(prod[:], acc[:], COPY)
            else:
                nc.vector.tensor_copy(prod[:], acc[:])
            prods.append(prod)
        half_list = O // 32
        nc.scalar.activation(pa[0][:].indirect(own[:]), prods[0][:], COPY)
        nc.vector.tensor_copy(pb[0][:].indirect(common[:]), prods[0][:])
        nc.scalar.activation(pa[1][:].indirect(own[:]), prods[1][:], COPY)
        nc.vector.tensor_copy(pb[1][:].indirect(common[:, :half_list]), prods[1][:, low])
        nc.scalar.activation(pb[1][:].indirect(common[:, half_list:]), prods[1][:, high], COPY)

        def add_and_store(m, cols, queue):
            y = keep.tile([P, cols.stop - cols.start], F32, name=f"y{m}_{cols.start}")
            nc.vector.tensor_tensor(y[:], pa[m][:, cols], pb[m][:, cols], ALU.add)
            queue.dma_start(out[m * P : (m + 1) * P, cols], y[:])

        add_and_store(0, slice(0, E), nc.sync)
        add_and_store(1, slice(0, E // 2), nc.sync)
        add_and_store(1, slice(E // 2, E), nc.scalar)
